import numpy as np
import ml_dtypes


def mxq(x, axis, fmt="e4m3"):
    dtype, down = {"e4m3": (ml_dtypes.float8_e4m3fn, 7), "e5m2": (ml_dtypes.float8_e5m2, 14)}[fmt]
    v = np.moveaxis(np.asarray(x, np.float32).astype(ml_dtypes.bfloat16).astype(np.float64), axis, -1)
    blocks = v.reshape(v.shape[:-1] + (-1, 32))
    amax = np.abs(blocks).max(-1, keepdims=True)
    byte = np.maximum(np.where(amax > 0, np.frexp(amax)[1] - 1 + 127, 0) - down, 1)
    scale = np.exp2(byte - 127.0)
    codes = (blocks / scale).astype(np.float32).astype(dtype).astype(np.float64)
    return np.moveaxis((codes * scale).reshape(v.shape), -1, axis)


WIDE = False


def mx_kscale(k):
    if not WIDE:
        return np.ones(k)
    levels = np.array([10, -10, 5, -5, 0])
    if k % 512:
        return np.exp2(np.random.permutation(np.resize(levels, k // 32))).repeat(32)
    a = np.empty((k // 512, 16))
    for p in range(k // 512):
        a[p, :8] = np.random.permutation(np.resize(levels, 8))
        for g in range(8):
            far = levels[np.abs(levels - a[p, g]) >= 10]
            a[p, g + 8] = far[np.random.randint(len(far))]
    return np.exp2(a.ravel()).repeat(32)


def f64(x):
    return np.asarray(x).astype(np.float64)


def striped(idx):
    return np.tile(idx.reshape(-1, 16).T, (8, 1)).astype(np.uint16)


def unstriped(offs):
    return offs[:16].T.reshape(-1).astype(np.int64)


def pack_weight(w):
    k, n = w.shape
    w = f64(np.asarray(w, np.float32).astype(ml_dtypes.bfloat16)).reshape(k // 32, 32, n)
    amax = np.abs(w).max(1)
    byte = np.clip(np.where(amax > 0, np.frexp(amax)[1] - 1 + 127 - 7, 1), 1, 254)
    scaled = (w * np.exp2(127.0 - byte)[:, None, :]).reshape(k, n).astype(np.float32)
    words = np.ascontiguousarray(scaled.reshape(k // 512, 128, 4, n).transpose(0, 1, 3, 2)).astype(ml_dtypes.float8_e4m3fn).view(np.uint8)
    return words, np.ascontiguousarray(byte.astype(np.uint8).reshape(k // 512, 16, n))


def unpack_weight(words, scales):
    g, p, n, _ = words.shape
    vals = np.ascontiguousarray(words).view(ml_dtypes.float8_e4m3fn).astype(np.float64) * np.repeat(np.exp2(scales.astype(np.float64) - 127.0), 8, axis=1)[..., None]
    return vals.transpose(0, 1, 3, 2).reshape(g * 512, n)


def sigmoid(v):
    return 1.0 / (1.0 + np.exp(-np.maximum(v, -700.0)))


K, T, S, V = 512, 2048, 1024, 512
P = 2 ** 7


def setup_inputs():
    n = np.random.standard_normal
    s = mx_kscale(K)[:, None]
    packed_xT = pack_weight(n((K, T)) * s)
    return {
        "x_words": packed_xT[0],
        "x_scales": packed_xT[1],
        "hT": (n((K, V)) / np.sqrt(K) / s).astype(np.float32),
        "rad": (np.tile(np.random.uniform(0.8, 1.6, T), (P, 1))).astype(np.float32),
        "rf": (np.tile(np.random.uniform(1.1, 1.6, T), (P, 1))).astype(np.float32),
        "qn": (np.random.uniform(0.8, 1.6, (V, 1))).astype(np.float32),
        "offs": striped(np.random.permutation(T)[:S]),
    }


def reference(x_words, x_scales, hT, rad, rf, qn, offs):
    hTq = mxq(f64(hT), 0, "e4m3")
    xq = unpack_weight(x_words, x_scales)[:, unstriped(offs)]
    y = hTq.T @ xq
    ip = f64(qn) * ((0.3 * (y * (f64(rad)[:1][:, unstriped(offs)]))) * (f64(rf)[:1][:, unstriped(offs)]))
    ds = (f64(rad)[:1][:, unstriped(offs)]) ** 2 - (2.0 * ip)
    er = f64(qn) * (0.3 * ((f64(rad)[:1][:, unstriped(offs)]) * (np.sqrt((f64(rf)[:1][:, unstriped(offs)]) ** 2 - 1.0))))
    ub = ds + er
    best = ub.min(axis=1, keepdims=True)
    return sigmoid(-3.0 * (ds - er - best))

@@ -1,0 +1,204 @@
+from contextlib import ExitStack
+
+import concourse.mybir as mybir
+from concourse.masks import make_identity
+
+K, T, S, V = 512, 2048, 1024, 512
+FLOPS = 2 * K * V * S
+
+F32 = mybir.dt.float32
+BF16 = mybir.dt.bfloat16
+I32 = mybir.dt.int32
+U32 = mybir.dt.uint32
+U16 = mybir.dt.uint16
+U8 = mybir.dt.uint8
+FP8X4 = mybir.dt.float8_e4m3fn_x4
+ALU = mybir.AluOpType
+ACT = mybir.ActivationFunctionType
+
+P = 128
+PACK = 4
+BANK = 512
+PIECE = 256
+GROUP = 256
+POOL_TILES = (0, 1, 2)
+
+
+def tile_picked_yrabit_soft_p_kernel(tc, x_words, x_scales, hT, rad, rf, qn, offs, out):
+    nc = tc.nc
+    n_j = S // P
+    n_t = V // P
+    with ExitStack() as ctx:
+        keep = ctx.enter_context(tc.tile_pool(name="keep", bufs=1))
+        ring = ctx.enter_context(tc.tile_pool(name="ring", bufs=6))
+        reuse = ctx.enter_context(tc.tile_pool(name="reuse", bufs=1))
+        psum_y = ctx.enter_context(tc.psum_pool(name="psum_y", bufs=3))
+        psum_t = ctx.enter_context(tc.psum_pool(name="psum_t", bufs=5))
+
+        offsets = keep.tile([P, S // 16], U16, name="offsets")
+        nc.sync.dma_start(offsets[:], offs)
+        h_view = hT.rearrange("(p j) t -> p j t", j=PACK)
+        h_raw = [keep.tile([P, PACK, GROUP], F32, name="h_raw0")]
+        nc.scalar.dma_start(h_raw[0][:], h_view[:, :, 0:GROUP])
+
+        planes = keep.tile([P, T], U8, name="planes")
+        nc.vector.memset(planes[:].bitcast(I32), 0)
+        for quad in range(4):
+            nc.sync.dma_start(planes[32 * quad : 32 * quad + 4, :].bitcast(I32), x_scales[0, 4 * quad : 4 * quad + 4, :].bitcast(I32))
+        rows = keep.tile([P, T], F32, name="rows")
+        nc.vector.memset(rows[:].bitcast(I32), 0)
+        nc.sync.dma_start(rows[0:1, :], rad[0:1, :])
+        nc.sync.dma_start(rows[1:2, :], rf[0:1, :])
+        q_flat = keep.tile([P, P], F32, name="q_flat")
+        nc.vector.memset(q_flat[:], 0.0)
+        nc.sync.dma_start(q_flat[0:n_t, :], qn.rearrange("(i p) o -> i (p o)", p=P))
+
+        ident = keep.tile([P, P], F32, name="ident")
+        make_identity(nc, ident[:])
+        warm = reuse.tile([P, 16], F32, name="warm", offset=16384 - 32)
+        nc.scalar.activation(warm[:], ident[:, 0:16], ACT.Sqrt)
+        h_raw.append(reuse.tile([P, PACK, GROUP], F32, name="h_raw1", offset=16384))
+        nc.scalar.dma_start(h_raw[1][:], h_view[:, :, GROUP:V])
+        words = reuse.tile([P, T], U32, name="words", offset=8192)
+        nc.scalar.dma_start(words[:].bitcast(I32), x_words[0].rearrange("p n r -> p (n r)").bitcast(I32))
+        q_turn = psum_t.tile([P, P], F32, tag="bank", name="q_turn")
+        nc.tensor.transpose(q_turn[:], q_flat[:], ident[:])
+        q_col = keep.tile([P, n_t], F32, name="q_col")
+        nc.scalar.copy(q_col[:], q_turn[:, 0:n_t])
+        q3_col = keep.tile([P, n_t], F32, name="q3_col")
+        nc.gpsimd.tensor_scalar(q3_col[:], q_col[:], 3.0, 0.0, ALU.mult, ALU.add)
+
+        q_bank = psum_t.tile([P, BANK], F32, tag="bank", name="q_bank")
+        for i in range(n_t):
+            nc.tensor.transpose(q_bank[:, i * P : (i + 1) * P], q_col[:, i : i + 1].to_broadcast([P, P]), ident[:])
+        q_row = keep.tile([P, V], F32, name="q_row")
+        nc.scalar.copy(q_row[:], q_bank[:])
+
+        picked = reuse.tile([P, n_j, 2], F32, name="picked", offset=20480, align_bytes=64)
+        for half in range(2):
+            got = reuse.tile([P, BANK], F32, name=f"got{half}", offset=2048 * half, align_bytes=64)
+            nc.vector.tensor_copy(got[:], rows[:].indirect(offsets[:, 32 * half : 32 * (half + 1)]))
+            bank = psum_t.tile([P, 4, P], F32, tag="bank", name=f"rf_bank{half}")
+            for c in range(4):
+                nc.tensor.transpose(bank[:, c, :], got[:, c * P : (c + 1) * P], ident[:])
+            nc.scalar.copy(picked[:, 4 * half : 4 * half + 4, :], bank[:, :, 0:2])
+        r_col, f_col = picked[:, :, 0], picked[:, :, 1]
+        squares = keep.tile([P, n_j, 2], F32, name="squares")
+        nc.scalar.activation(squares[:], picked[:], ACT.Square)
+        root = reuse.tile([P, n_j], F32, name="root", offset=4096, align_bytes=64)
+        nc.scalar.activation(root[:], squares[:, :, 1], ACT.Sqrt, bias=-1.0)
+        warm2 = keep.tile([P, 1], F32, name="warm2")
+        nc.scalar.activation(warm2[:], root[:, 0:1], ACT.Sigmoid)
+        f_inv = reuse.tile([P, n_j], F32, name="f_inv", offset=5120, align_bytes=64)
+        nc.vector.reciprocal(f_inv[:], f_col)
+        slope = keep.tile([P, n_j], F32, name="slope")
+        nc.vector.scalar_tensor_tensor(slope[:], r_col, -0.6, f_col, ALU.mult, ALU.mult)
+        gap = keep.tile([P, n_j], F32, name="gap")
+        nc.vector.scalar_tensor_tensor(gap[:], root[:], -0.6, r_col, ALU.mult, ALU.mult)
+        shift = keep.tile([P, n_j], F32, name="shift")
+        nc.vector.scalar_tensor_tensor(shift[:], root[:], 0.5, f_inv[:], ALU.mult, ALU.mult)
+
+        h_codes, h_scales = [], []
+        for g in range(V // GROUP):
+            grouped = keep.tile([P, GROUP, PACK], BF16, name=f"grouped{g}", align_bytes=64)
+            nc.scalar.copy(
+                grouped[:].rearrange("p (c i) j -> p c j i", i=4),
+                h_raw[g][:].rearrange("p j (c i) -> p c j i", i=4),
+            )
+            codes = reuse.tile([P, GROUP], U32, name=f"h_codes{g}", offset=(0, 6144)[g], align_bytes=64)
+            scales = reuse.tile([P, GROUP], U8, name=f"h_scales{g}", offset=(1536, 1792)[g], align_bytes=64)
+            nc.vector.quantize_mx(out=codes[:].bitcast(FP8X4), scales=scales[:], in_=grouped[:].rearrange("p t j -> p (t j)"))
+            h_codes.append(codes)
+            h_scales.append(scales)
+
+        x_codes, x_planes = [], []
+        for piece in range(S // PIECE):
+            cut = offsets[:, piece * (PIECE // 16) : (piece + 1) * (PIECE // 16)]
+            plane = reuse.tile([P, PIECE], U8, name=f"x_plane{piece}", offset=(7168, 7424, 1024, 1280)[piece], align_bytes=64)
+            nc.vector.tensor_copy(plane[:], planes[:].indirect(cut))
+            code = reuse.tile([P, PIECE], U32, name=f"x_code{piece}", offset=(2048, 20480, 4096, 5120)[piece], align_bytes=64)
+            nc.vector.tensor_copy(code[:], words[:].indirect(cut))
+            x_codes.append(code)
+            x_planes.append(plane)
+
+        gap_row = keep.tile([P, S], F32, name="gap_row")
+        for half in range(2):
+            bank = psum_t.tile([P, 4, P], F32, tag="bank", name=f"gap_bank{half}")
+            for c in range(4):
+                jt = 4 * half + c
+                nc.tensor.transpose(bank[:, c, :], gap[:, jt : jt + 1].to_broadcast([P, P]), ident[:])
+            nc.scalar.copy(gap_row[:, half * BANK : (half + 1) * BANK], bank[:].rearrange("p c n -> p (c n)"))
+        drop = {}
+        for tt in POOL_TILES:
+            drop[tt] = keep.tile([P, S], F32, name=f"drop{tt}")
+        for tt, half in ((0, 0), (1, 0), (0, 1), (1, 1), (2, 0), (2, 1), (3, 0), (3, 1)):
+            if tt in POOL_TILES:
+                cols = slice(half * BANK, (half + 1) * BANK)
+                nc.gpsimd.tensor_scalar(drop[tt][:, cols], gap_row[:, cols], q3_col[:, tt : tt + 1], 0.0, ALU.mult, ALU.add)
+
+        best = [[keep.tile([P, 1], F32, name=f"best{tt}_{half}") for half in range(2)] for tt in range(n_t)]
+        lower = {}
+
+        def upper_bounds(g, half):
+            banks = [psum_t.tile([P, 4, P], F32, tag="bank", name=f"ub{g}_{half}_{u}") for u in range(2)]
+            for pair in range(2):
+                piece = 2 * half + pair
+                y = psum_y.tile([P, 2, GROUP], F32, tag="y", name=f"y{g}_{piece}")
+                for u in range(2):
+                    cols = slice(u * P, (u + 1) * P)
+                    nc.tensor.matmul_mx(
+                        out=y[:, u, :],
+                        lhsT=x_codes[piece][:, cols].bitcast(FP8X4),
+                        lhsT_scale=x_planes[piece][:, cols],
+                        rhs=h_codes[g][:].bitcast(FP8X4),
+                        rhs_scale=h_scales[g][:],
+                        start=True,
+                        stop=True,
+                    )
+                for u in range(2):
+                    jt = 2 * piece + u
+                    z = ring.tile([P, GROUP], F32, tag="z", name=f"z{g}_{jt}")
+                    nc.vector.scalar_tensor_tensor(
+                        z[:], y[:, u, :], shift[:, jt : jt + 1], q_row[:, g * GROUP : (g + 1) * GROUP], ALU.subtract, ALU.mult
+                    )
+                    ub_t = ring.tile([P, GROUP], F32, tag="ub_t", name=f"ub_t{g}_{jt}")
+                    nc.scalar.activation(ub_t[:], z[:], ACT.Identity, bias=squares[:, jt, 0:1], scale=slope[:, jt : jt + 1])
+                    for w in range(2):
+                        nc.tensor.transpose(banks[w][:, jt % 4, :], ub_t[:, w * P : (w + 1) * P], ident[:])
+            return banks
+
+        def lower_bounds(g, half, banks):
+            cols = slice(half * BANK, (half + 1) * BANK)
+            for w in range(2):
+                tt = 2 * g + w
+                ub = banks[w][:].rearrange("p c n -> p (c n)")
+                low = keep.tile([P, BANK], F32, name=f"low{tt}_{half}")
+                lower[tt, half] = low
+                if tt not in POOL_TILES:
+                    nc.vector.scalar_tensor_tensor(low[:], gap_row[:, cols], q_col[:, tt : tt + 1], ub, ALU.mult, ALU.add)
+                ub3 = ring.tile([P, BANK], F32, tag="ub3", name=f"ub3_{tt}_{half}")
+                nc.vector.tensor_scalar(ub3[:], ub, 3.0, best[tt][0][:] if half else None, ALU.mult, ALU.min, accum_out=best[tt][half][:])
+                if tt in POOL_TILES:
+                    nc.gpsimd.tensor_tensor(low[:], ub3[:], drop[tt][:, cols], ALU.add)
+
+        def finish(g):
+            for w in range(2):
+                tt = 2 * g + w
+                for half in range(2):
+                    res = ring.tile([P, BANK], F32, tag="res", name=f"res{tt}_{half}")
+                    nc.scalar.activation(
+                        res[:], lower[tt, half][:], ACT.Sigmoid, bias=best[tt][1][:], scale=-1.0 if tt in POOL_TILES else -3.0
+                    )
+                    nc.sync.dma_start(out[tt * P : (tt + 1) * P, half * BANK : (half + 1) * BANK], res[:])
+
+        units = [(g, half) for g in range(V // GROUP) for half in range(2)]
+        waiting = None
+        for unit in units:
+            banks = upper_bounds(*unit)
+            if waiting is not None:
+                lower_bounds(*waiting)
+                if waiting[1] == 1:
+                    finish(waiting[0])
+            waiting = (*unit, banks)
+        lower_bounds(*waiting)
+        finish(waiting[0])

@@ -21,7 +21,7 @@ PACK = 4
 BANK = 512
 PIECE = 256
 GROUP = 256
-POOL_TILES = (0, 1, 2)
+POOL_TILES = ()
 
 
 def tile_picked_yrabit_soft_p_kernel(tc, x_words, x_scales, hT, rad, rf, qn, offs, out):
@@ -46,27 +46,22 @@ def tile_picked_yrabit_soft_p_kernel(tc, x_words, x_scales, hT, rad, rf, qn, off
         for quad in range(4):
             nc.sync.dma_start(planes[32 * quad : 32 * quad + 4, :].bitcast(I32), x_scales[0, 4 * quad : 4 * quad + 4, :].bitcast(I32))
         rows = keep.tile([P, T], F32, name="rows")
-        nc.vector.memset(rows[:].bitcast(I32), 0)
+        nc.vector.memset(rows[:, 0 : T // 2].bitcast(I32), 0)
+        nc.gpsimd.memset(rows[:, T // 2 : T].bitcast(I32), 0)
         nc.sync.dma_start(rows[0:1, :], rad[0:1, :])
         nc.sync.dma_start(rows[1:2, :], rf[0:1, :])
-        q_flat = keep.tile([P, P], F32, name="q_flat")
-        nc.vector.memset(q_flat[:], 0.0)
-        nc.sync.dma_start(q_flat[0:n_t, :], qn.rearrange("(i p) o -> i (p o)", p=P))
 
         ident = keep.tile([P, P], F32, name="ident")
         make_identity(nc, ident[:])
+        q_col = keep.tile([P, n_t], F32, name="q_col")
+        with nc.allow_non_contiguous_dma(reason="one query norm a partition"):
+            nc.gpsimd.dma_start(q_col[:], qn.rearrange("(i p) o -> p (i o)", p=P))
         warm = reuse.tile([P, 16], F32, name="warm", offset=16384 - 32)
         nc.scalar.activation(warm[:], ident[:, 0:16], ACT.Sqrt)
         h_raw.append(reuse.tile([P, PACK, GROUP], F32, name="h_raw1", offset=16384))
         nc.scalar.dma_start(h_raw[1][:], h_view[:, :, GROUP:V])
         words = reuse.tile([P, T], U32, name="words", offset=8192)
         nc.scalar.dma_start(words[:].bitcast(I32), x_words[0].rearrange("p n r -> p (n r)").bitcast(I32))
-        q_turn = psum_t.tile([P, P], F32, tag="bank", name="q_turn")
-        nc.tensor.transpose(q_turn[:], q_flat[:], ident[:])
-        q_col = keep.tile([P, n_t], F32, name="q_col")
-        nc.scalar.copy(q_col[:], q_turn[:, 0:n_t])
-        q3_col = keep.tile([P, n_t], F32, name="q3_col")
-        nc.gpsimd.tensor_scalar(q3_col[:], q_col[:], 3.0, 0.0, ALU.mult, ALU.add)
 
         q_bank = psum_t.tile([P, BANK], F32, tag="bank", name="q_bank")
         for i in range(n_t):
@@ -74,7 +69,7 @@ def tile_picked_yrabit_soft_p_kernel(tc, x_words, x_scales, hT, rad, rf, qn, off
         q_row = keep.tile([P, V], F32, name="q_row")
         nc.scalar.copy(q_row[:], q_bank[:])
 
-        picked = reuse.tile([P, n_j, 2], F32, name="picked", offset=20480, align_bytes=64)
+        picked = reuse.tile([P, n_j, 2], F32, name="picked", offset=16384, align_bytes=64)
         for half in range(2):
             got = reuse.tile([P, BANK], F32, name=f"got{half}", offset=2048 * half, align_bytes=64)
             nc.vector.tensor_copy(got[:], rows[:].indirect(offsets[:, 32 * half : 32 * (half + 1)]))
@@ -116,25 +111,20 @@ def tile_picked_yrabit_soft_p_kernel(tc, x_words, x_scales, hT, rad, rf, qn, off
             cut = offsets[:, piece * (PIECE // 16) : (piece + 1) * (PIECE // 16)]
             plane = reuse.tile([P, PIECE], U8, name=f"x_plane{piece}", offset=(7168, 7424, 1024, 1280)[piece], align_bytes=64)
             nc.vector.tensor_copy(plane[:], planes[:].indirect(cut))
-            code = reuse.tile([P, PIECE], U32, name=f"x_code{piece}", offset=(2048, 20480, 4096, 5120)[piece], align_bytes=64)
+            code = reuse.tile([P, PIECE], U32, name=f"x_code{piece}", offset=(2048, 16384, 4096, 5120)[piece], align_bytes=64)
             nc.vector.tensor_copy(code[:], words[:].indirect(cut))
             x_codes.append(code)
             x_planes.append(plane)
 
         gap_row = keep.tile([P, S], F32, name="gap_row")
-        for half in range(2):
-            bank = psum_t.tile([P, 4, P], F32, tag="bank", name=f"gap_bank{half}")
-            for c in range(4):
-                jt = 4 * half + c
-                nc.tensor.transpose(bank[:, c, :], gap[:, jt : jt + 1].to_broadcast([P, P]), ident[:])
-            nc.scalar.copy(gap_row[:, half * BANK : (half + 1) * BANK], bank[:].rearrange("p c n -> p (c n)"))
-        drop = {}
-        for tt in POOL_TILES:
-            drop[tt] = keep.tile([P, S], F32, name=f"drop{tt}")
-        for tt, half in ((0, 0), (1, 0), (0, 1), (1, 1), (2, 0), (2, 1), (3, 0), (3, 1)):
-            if tt in POOL_TILES:
-                cols = slice(half * BANK, (half + 1) * BANK)
-                nc.gpsimd.tensor_scalar(drop[tt][:, cols], gap_row[:, cols], q3_col[:, tt : tt + 1], 0.0, ALU.mult, ALU.add)
+
+        def spread_gap():
+            for half in range(2):
+                bank = psum_t.tile([P, 4, P], F32, tag="bank", name=f"gap_bank{half}")
+                for c in range(4):
+                    jt = 4 * half + c
+                    nc.tensor.transpose(bank[:, c, :], gap[:, jt : jt + 1].to_broadcast([P, P]), ident[:])
+                nc.scalar.copy(gap_row[:, half * BANK : (half + 1) * BANK], bank[:].rearrange("p c n -> p (c n)"))
 
         best = [[keep.tile([P, 1], F32, name=f"best{tt}_{half}") for half in range(2)] for tt in range(n_t)]
         lower = {}
@@ -178,8 +168,6 @@ def tile_picked_yrabit_soft_p_kernel(tc, x_words, x_scales, hT, rad, rf, qn, off
                     nc.vector.scalar_tensor_tensor(low[:], gap_row[:, cols], q_col[:, tt : tt + 1], ub, ALU.mult, ALU.add)
                 ub3 = ring.tile([P, BANK], F32, tag="ub3", name=f"ub3_{tt}_{half}")
                 nc.vector.tensor_scalar(ub3[:], ub, 3.0, best[tt][0][:] if half else None, ALU.mult, ALU.min, accum_out=best[tt][half][:])
-                if tt in POOL_TILES:
-                    nc.gpsimd.tensor_tensor(low[:], ub3[:], drop[tt][:, cols], ALU.add)
 
         def finish(g):
             for w in range(2):
@@ -195,6 +183,8 @@ def tile_picked_yrabit_soft_p_kernel(tc, x_words, x_scales, hT, rad, rf, qn, off
         waiting = None
         for unit in units:
             banks = upper_bounds(*unit)
+            if waiting is None:
+                spread_gap()
             if waiting is not None:
                 lower_bounds(*waiting)
                 if waiting[1] == 1:

@@ -20,8 +20,8 @@ P = 128
 PACK = 4
 BANK = 512
 PIECE = 256
-GROUP = 256
-POOL_TILES = ()
+POOL_HALVES = ((0, 0), (1, 0), (0, 1), (1, 1), (2, 0))
+SCALAR_DROPS = ((0, 1), (1, 1))
 
 
 def tile_picked_yrabit_soft_p_kernel(tc, x_words, x_scales, hT, rad, rf, qn, offs, out):
@@ -33,50 +33,79 @@ def tile_picked_yrabit_soft_p_kernel(tc, x_words, x_scales, hT, rad, rf, qn, off
         ring = ctx.enter_context(tc.tile_pool(name="ring", bufs=6))
         reuse = ctx.enter_context(tc.tile_pool(name="reuse", bufs=1))
         psum_y = ctx.enter_context(tc.psum_pool(name="psum_y", bufs=3))
-        psum_t = ctx.enter_context(tc.psum_pool(name="psum_t", bufs=5))
+        psum_t = ctx.enter_context(tc.psum_pool(name="psum_t", bufs=1))
 
         offsets = keep.tile([P, S // 16], U16, name="offsets")
         nc.sync.dma_start(offsets[:], offs)
-        h_view = hT.rearrange("(p j) t -> p j t", j=PACK)
-        h_raw = [keep.tile([P, PACK, GROUP], F32, name="h_raw0")]
-        nc.scalar.dma_start(h_raw[0][:], h_view[:, :, 0:GROUP])
+        q_flat = keep.tile([P, P], F32, name="q_flat")
+        nc.vector.memset(q_flat[:], 0.0)
+        nc.sync.dma_start(q_flat[0:n_t, :], qn.rearrange("(i p) o -> i (p o)", p=P))
+        h_raw = reuse.tile([P, PACK, V], F32, name="h_raw", offset=16384)
+        nc.scalar.dma_start(h_raw[:], hT.rearrange("(p j) t -> p j t", j=PACK))
 
         planes = keep.tile([P, T], U8, name="planes")
         nc.vector.memset(planes[:].bitcast(I32), 0)
         for quad in range(4):
             nc.sync.dma_start(planes[32 * quad : 32 * quad + 4, :].bitcast(I32), x_scales[0, 4 * quad : 4 * quad + 4, :].bitcast(I32))
         rows = keep.tile([P, T], F32, name="rows")
-        nc.vector.memset(rows[:, 0 : T // 2].bitcast(I32), 0)
-        nc.gpsimd.memset(rows[:, T // 2 : T].bitcast(I32), 0)
-        nc.sync.dma_start(rows[0:1, :], rad[0:1, :])
-        nc.sync.dma_start(rows[1:2, :], rf[0:1, :])
+        nc.vector.memset(rows[:].bitcast(I32), 0)
+        nc.sync.dma_start(rows[8:9, :], rad[0:1, :])
+        nc.sync.dma_start(rows[72:73, :], rf[0:1, :])
 
         ident = keep.tile([P, P], F32, name="ident")
         make_identity(nc, ident[:])
-        q_col = keep.tile([P, n_t], F32, name="q_col")
-        with nc.allow_non_contiguous_dma(reason="one query norm a partition"):
-            nc.gpsimd.dma_start(q_col[:], qn.rearrange("(i p) o -> p (i o)", p=P))
-        warm = reuse.tile([P, 16], F32, name="warm", offset=16384 - 32)
-        nc.scalar.activation(warm[:], ident[:, 0:16], ACT.Sqrt)
-        h_raw.append(reuse.tile([P, PACK, GROUP], F32, name="h_raw1", offset=16384))
-        nc.scalar.dma_start(h_raw[1][:], h_view[:, :, GROUP:V])
-        words = reuse.tile([P, T], U32, name="words", offset=8192)
+        seed = keep.tile([P, 16], F32, name="seed")
+        nc.vector.memset(seed[:], 1.0)
+        warm = reuse.tile([P, 16], F32, name="warm", offset=16384 - 64)
+        nc.scalar.activation(warm[:], seed[:], ACT.Sqrt)
+        words = reuse.tile([P, T], U32, name="words", offset=8192 - 32)
         nc.scalar.dma_start(words[:].bitcast(I32), x_words[0].rearrange("p n r -> p (n r)").bitcast(I32))
 
-        q_bank = psum_t.tile([P, BANK], F32, tag="bank", name="q_bank")
+        q_turn = psum_t.tile([P, P], F32, tag="bank4", name="q_turn")
+        nc.tensor.transpose(q_turn[:], q_flat[:], ident[:])
+        q_col = keep.tile([P, n_t], F32, name="q_col")
+        nc.scalar.copy(q_col[:], q_turn[:, 0:n_t])
+        grouped = keep.tile([P, V, PACK], BF16, name="grouped", align_bytes=64)
+        nc.scalar.copy(grouped[:].rearrange("p (c i) j -> p c j i", i=4), h_raw[:].rearrange("p j (c i) -> p c j i", i=4))
+
+        q_bank = psum_t.tile([P, BANK], F32, tag="bank0", name="q_bank")
         for i in range(n_t):
             nc.tensor.transpose(q_bank[:, i * P : (i + 1) * P], q_col[:, i : i + 1].to_broadcast([P, P]), ident[:])
         q_row = keep.tile([P, V], F32, name="q_row")
         nc.scalar.copy(q_row[:], q_bank[:])
+        q3_col = keep.tile([P, n_t], F32, name="q3_col")
+        nc.scalar.activation(q3_col[:], q_col[:], ACT.Copy, scale=3.0)
 
+        x_codes, x_planes = {}, {}
+
+        def entries(piece):
+            return offsets[:, piece * (PIECE // 16) : (piece + 1) * (PIECE // 16)]
+
+        def pick_planes(piece):
+            x_planes[piece] = reuse.tile([P, PIECE], U8, name=f"x_plane{piece}", offset=(6144, 6400, 0, 256)[piece], align_bytes=64)
+            nc.vector.tensor_copy(x_planes[piece][:], planes[:].indirect(entries(piece)))
+
+        def pick_codes(piece):
+            x_codes[piece] = reuse.tile([P, PIECE], U32, name=f"x_code{piece}", offset=(1024, 16384, 4096, 5120)[piece], align_bytes=64)
+            nc.vector.tensor_copy(x_codes[piece][:], words[:].indirect(entries(piece)))
+
+        pick_planes(0)
+        pick_planes(1)
         picked = reuse.tile([P, n_j, 2], F32, name="picked", offset=16384, align_bytes=64)
         for half in range(2):
             got = reuse.tile([P, BANK], F32, name=f"got{half}", offset=2048 * half, align_bytes=64)
             nc.vector.tensor_copy(got[:], rows[:].indirect(offsets[:, 32 * half : 32 * (half + 1)]))
-            bank = psum_t.tile([P, 4, P], F32, tag="bank", name=f"rf_bank{half}")
+            bank = psum_t.tile([P, 4, P], F32, tag=f"bank{1 + half}", name=f"rf_bank{half}")
             for c in range(4):
                 nc.tensor.transpose(bank[:, c, :], got[:, c * P : (c + 1) * P], ident[:])
-            nc.scalar.copy(picked[:, 4 * half : 4 * half + 4, :], bank[:, :, 0:2])
+            nc.scalar.copy(picked[:, 4 * half : 4 * half + 4, :], bank[:, :, 8:73:64])
+        pick_planes(2)
+        pick_planes(3)
+        h_codes = reuse.tile([P, V], U32, name="h_codes", offset=2048, align_bytes=64)
+        h_scales = reuse.tile([P, V], U8, name="h_scales", offset=6656, align_bytes=64)
+        nc.vector.quantize_mx(out=h_codes[:].bitcast(FP8X4), scales=h_scales[:], in_=grouped[:].rearrange("p t j -> p (t j)"))
+        pick_codes(0)
+
         r_col, f_col = picked[:, :, 0], picked[:, :, 1]
         squares = keep.tile([P, n_j, 2], F32, name="squares")
         nc.scalar.activation(squares[:], picked[:], ACT.Square)
@@ -93,102 +122,96 @@ def tile_picked_yrabit_soft_p_kernel(tc, x_words, x_scales, hT, rad, rf, qn, off
         shift = keep.tile([P, n_j], F32, name="shift")
         nc.vector.scalar_tensor_tensor(shift[:], root[:], 0.5, f_inv[:], ALU.mult, ALU.mult)
 
-        h_codes, h_scales = [], []
-        for g in range(V // GROUP):
-            grouped = keep.tile([P, GROUP, PACK], BF16, name=f"grouped{g}", align_bytes=64)
-            nc.scalar.copy(
-                grouped[:].rearrange("p (c i) j -> p c j i", i=4),
-                h_raw[g][:].rearrange("p j (c i) -> p c j i", i=4),
-            )
-            codes = reuse.tile([P, GROUP], U32, name=f"h_codes{g}", offset=(0, 6144)[g], align_bytes=64)
-            scales = reuse.tile([P, GROUP], U8, name=f"h_scales{g}", offset=(1536, 1792)[g], align_bytes=64)
-            nc.vector.quantize_mx(out=codes[:].bitcast(FP8X4), scales=scales[:], in_=grouped[:].rearrange("p t j -> p (t j)"))
-            h_codes.append(codes)
-            h_scales.append(scales)
-
-        x_codes, x_planes = [], []
-        for piece in range(S // PIECE):
-            cut = offsets[:, piece * (PIECE // 16) : (piece + 1) * (PIECE // 16)]
-            plane = reuse.tile([P, PIECE], U8, name=f"x_plane{piece}", offset=(7168, 7424, 1024, 1280)[piece], align_bytes=64)
-            nc.vector.tensor_copy(plane[:], planes[:].indirect(cut))
-            code = reuse.tile([P, PIECE], U32, name=f"x_code{piece}", offset=(2048, 16384, 4096, 5120)[piece], align_bytes=64)
-            nc.vector.tensor_copy(code[:], words[:].indirect(cut))
-            x_codes.append(code)
-            x_planes.append(plane)
-
         gap_row = keep.tile([P, S], F32, name="gap_row")
 
-        def spread_gap():
-            for half in range(2):
-                bank = psum_t.tile([P, 4, P], F32, tag="bank", name=f"gap_bank{half}")
-                for c in range(4):
-                    jt = 4 * half + c
-                    nc.tensor.transpose(bank[:, c, :], gap[:, jt : jt + 1].to_broadcast([P, P]), ident[:])
-                nc.scalar.copy(gap_row[:, half * BANK : (half + 1) * BANK], bank[:].rearrange("p c n -> p (c n)"))
+        def spread_gap(half):
+            bank = psum_t.tile([P, 4, P], F32, tag="bank3", name=f"gap_bank{half}")
+            for c in range(4):
+                jt = 4 * half + c
+                nc.tensor.transpose(bank[:, c, :], gap[:, jt : jt + 1].to_broadcast([P, P]), ident[:])
+            nc.scalar.copy(gap_row[:, half * BANK : (half + 1) * BANK], bank[:].rearrange("p c n -> p (c n)"))
 
         best = [[keep.tile([P, 1], F32, name=f"best{tt}_{half}") for half in range(2)] for tt in range(n_t)]
-        lower = {}
+        upper, lower, drop = {}, {}, {}
 
-        def upper_bounds(g, half):
-            banks = [psum_t.tile([P, 4, P], F32, tag="bank", name=f"ub{g}_{half}_{u}") for u in range(2)]
-            for pair in range(2):
-                piece = 2 * half + pair
-                y = psum_y.tile([P, 2, GROUP], F32, tag="y", name=f"y{g}_{piece}")
-                for u in range(2):
-                    cols = slice(u * P, (u + 1) * P)
-                    nc.tensor.matmul_mx(
-                        out=y[:, u, :],
-                        lhsT=x_codes[piece][:, cols].bitcast(FP8X4),
-                        lhsT_scale=x_planes[piece][:, cols],
-                        rhs=h_codes[g][:].bitcast(FP8X4),
-                        rhs_scale=h_scales[g][:],
-                        start=True,
-                        stop=True,
-                    )
-                for u in range(2):
-                    jt = 2 * piece + u
-                    z = ring.tile([P, GROUP], F32, tag="z", name=f"z{g}_{jt}")
-                    nc.vector.scalar_tensor_tensor(
-                        z[:], y[:, u, :], shift[:, jt : jt + 1], q_row[:, g * GROUP : (g + 1) * GROUP], ALU.subtract, ALU.mult
-                    )
-                    ub_t = ring.tile([P, GROUP], F32, tag="ub_t", name=f"ub_t{g}_{jt}")
-                    nc.scalar.activation(ub_t[:], z[:], ACT.Identity, bias=squares[:, jt, 0:1], scale=slope[:, jt : jt + 1])
-                    for w in range(2):
-                        nc.tensor.transpose(banks[w][:, jt % 4, :], ub_t[:, w * P : (w + 1) * P], ident[:])
-            return banks
+        def make_drop(tt, half):
+            if (tt, half) in POOL_HALVES:
+                cols = slice(half * BANK, (half + 1) * BANK)
+                drop[tt, half] = keep.tile([P, BANK], F32, name=f"drop{tt}_{half}")
+                if (tt, half) in SCALAR_DROPS:
+                    nc.scalar.activation(drop[tt, half][:], gap_row[:, cols], ACT.Identity, scale=q3_col[:, tt : tt + 1])
+                else:
+                    nc.gpsimd.tensor_scalar(drop[tt, half][:], gap_row[:, cols], q3_col[:, tt : tt + 1], 0.0, ALU.mult, ALU.add)
 
-        def lower_bounds(g, half, banks):
+        def upper_bounds(code_tiles, query_tiles):
+            width = len(query_tiles) * P
+            queries = slice(query_tiles[0] * P, query_tiles[0] * P + width)
+            y = psum_y.tile([P, len(code_tiles), width], F32, tag="y", name=f"y{code_tiles[0]}_{query_tiles[0]}")
+            for u, jt in enumerate(code_tiles):
+                piece, cols = jt // 2, slice((jt % 2) * P, (jt % 2 + 1) * P)
+                nc.tensor.matmul_mx(
+                    out=y[:, u, :],
+                    lhsT=x_codes[piece][:, cols].bitcast(FP8X4),
+                    lhsT_scale=x_planes[piece][:, cols],
+                    rhs=h_codes[:, queries].bitcast(FP8X4),
+                    rhs_scale=h_scales[:, queries],
+                    start=True,
+                    stop=True,
+                )
+            for u, jt in enumerate(code_tiles):
+                z = ring.tile([P, width], F32, tag="z", name=f"z{jt}_{query_tiles[0]}")
+                nc.vector.scalar_tensor_tensor(z[:], y[:, u, :], shift[:, jt : jt + 1], q_row[:, queries], ALU.subtract, ALU.mult)
+                ub_t = ring.tile([P, width], F32, tag="ub_t", name=f"ub_t{jt}_{query_tiles[0]}")
+                nc.scalar.activation(ub_t[:], z[:], ACT.Identity, bias=squares[:, jt, 0:1], scale=slope[:, jt : jt + 1])
+                for w, tt in enumerate(query_tiles):
+                    if jt % 4 == 0:
+                        upper[tt, jt // 4] = psum_t.tile([P, 4, P], F32, tag=f"bank{((4, 0, 1, 2), (3, 4, 0, 3))[jt // 4][tt]}", name=f"ub{tt}_{jt // 4}")
+                    nc.tensor.transpose(upper[tt, jt // 4][:, jt % 4, :], ub_t[:, w * P : (w + 1) * P], ident[:])
+
+        def lower_bounds(tt, half):
             cols = slice(half * BANK, (half + 1) * BANK)
-            for w in range(2):
-                tt = 2 * g + w
-                ub = banks[w][:].rearrange("p c n -> p (c n)")
-                low = keep.tile([P, BANK], F32, name=f"low{tt}_{half}")
-                lower[tt, half] = low
-                if tt not in POOL_TILES:
-                    nc.vector.scalar_tensor_tensor(low[:], gap_row[:, cols], q_col[:, tt : tt + 1], ub, ALU.mult, ALU.add)
-                ub3 = ring.tile([P, BANK], F32, tag="ub3", name=f"ub3_{tt}_{half}")
-                nc.vector.tensor_scalar(ub3[:], ub, 3.0, best[tt][0][:] if half else None, ALU.mult, ALU.min, accum_out=best[tt][half][:])
+            ub = upper[tt, half][:].rearrange("p c n -> p (c n)")
+            low = keep.tile([P, BANK], F32, name=f"low{tt}_{half}")
+            lower[tt, half] = low
+            if (tt, half) not in POOL_HALVES:
+                nc.vector.scalar_tensor_tensor(low[:], gap_row[:, cols], q_col[:, tt : tt + 1], ub, ALU.mult, ALU.add)
+            ub3 = ring.tile([P, BANK], F32, tag="ub3", name=f"ub3_{tt}_{half}")
+            nc.vector.tensor_scalar(ub3[:], ub, 3.0, best[tt][0][:] if half else None, ALU.mult, ALU.min, accum_out=best[tt][half][:])
+            if (tt, half) in POOL_HALVES:
+                nc.gpsimd.tensor_tensor(low[:], ub3[:], drop[tt, half][:], ALU.add)
 
-        def finish(g):
-            for w in range(2):
-                tt = 2 * g + w
-                for half in range(2):
-                    res = ring.tile([P, BANK], F32, tag="res", name=f"res{tt}_{half}")
-                    nc.scalar.activation(
-                        res[:], lower[tt, half][:], ACT.Sigmoid, bias=best[tt][1][:], scale=-1.0 if tt in POOL_TILES else -3.0
-                    )
-                    nc.sync.dma_start(out[tt * P : (tt + 1) * P, half * BANK : (half + 1) * BANK], res[:])
+        def finish(tt, halves):
+            for half in halves:
+                res = ring.tile([P, BANK], F32, tag="res", name=f"res{tt}_{half}")
+                nc.scalar.activation(
+                    res[:], lower[tt, half][:], ACT.Sigmoid, bias=best[tt][1][:], scale=-1.0 if (tt, half) in POOL_HALVES else -3.0
+                )
+                nc.sync.dma_start(out[tt * P : (tt + 1) * P, half * BANK : (half + 1) * BANK], res[:])
 
-        units = [(g, half) for g in range(V // GROUP) for half in range(2)]
-        waiting = None
-        for unit in units:
-            banks = upper_bounds(*unit)
-            if waiting is None:
-                spread_gap()
-            if waiting is not None:
-                lower_bounds(*waiting)
-                if waiting[1] == 1:
-                    finish(waiting[0])
-            waiting = (*unit, banks)
-        lower_bounds(*waiting)
-        finish(waiting[0])
+        pick_codes(1)
+        spread_gap(0)
+        make_drop(0, 0)
+        make_drop(1, 0)
+        make_drop(2, 0)
+        for jt in range(4):
+            if jt == 2:
+                pick_codes(2)
+            upper_bounds((jt,), (0, 1, 2, 3))
+        spread_gap(1)
+        pick_codes(3)
+        for pair in ((4, 5), (6, 7)):
+            upper_bounds(pair, (0, 1))
+        make_drop(0, 1)
+        lower_bounds(0, 0)
+        lower_bounds(1, 0)
+        make_drop(1, 1)
+        for pair in ((4, 5), (6, 7)):
+            upper_bounds(pair, (2, 3))
+        for tt in (0, 1):
+            lower_bounds(tt, 1)
+            finish(tt, (0, 1))
+        lower_bounds(2, 0)
+        lower_bounds(3, 0)
+        for tt in (2, 3):
+            lower_bounds(tt, 1)
+            finish(tt, (1, 0))

from contextlib import ExitStack

import concourse.mybir as mybir
from concourse.masks import make_identity

K, T, S, V = 512, 2048, 1024, 512
FLOPS = 2 * K * V * S

F32 = mybir.dt.float32
BF16 = mybir.dt.bfloat16
I32 = mybir.dt.int32
U32 = mybir.dt.uint32
U16 = mybir.dt.uint16
U8 = mybir.dt.uint8
FP8X4 = mybir.dt.float8_e4m3fn_x4
ALU = mybir.AluOpType
ACT = mybir.ActivationFunctionType

P = 128
PACK = 4
BANK = 512
PIECE = 256
POOL_HALVES = ((0, 0), (1, 0), (0, 1), (1, 1), (2, 0))
SCALAR_DROPS = ((0, 1), (1, 1))


def tile_picked_yrabit_soft_p_kernel(tc, x_words, x_scales, hT, rad, rf, qn, offs, out):
    nc = tc.nc
    n_j = S // P
    n_t = V // P
    with ExitStack() as ctx:
        keep = ctx.enter_context(tc.tile_pool(name="keep", bufs=1))
        ring = ctx.enter_context(tc.tile_pool(name="ring", bufs=6))
        reuse = ctx.enter_context(tc.tile_pool(name="reuse", bufs=1))
        psum_y = ctx.enter_context(tc.psum_pool(name="psum_y", bufs=3))
        psum_t = ctx.enter_context(tc.psum_pool(name="psum_t", bufs=1))

        offsets = keep.tile([P, S // 16], U16, name="offsets")
        nc.sync.dma_start(offsets[:], offs)
        q_flat = keep.tile([P, P], F32, name="q_flat")
        nc.vector.memset(q_flat[:], 0.0)
        nc.sync.dma_start(q_flat[0:n_t, :], qn.rearrange("(i p) o -> i (p o)", p=P))
        h_raw = reuse.tile([P, PACK, V], F32, name="h_raw", offset=16384)
        nc.scalar.dma_start(h_raw[:], hT.rearrange("(p j) t -> p j t", j=PACK))

        planes = keep.tile([P, T], U8, name="planes")
        nc.vector.memset(planes[:].bitcast(I32), 0)
        for quad in range(4):
            nc.sync.dma_start(planes[32 * quad : 32 * quad + 4, :].bitcast(I32), x_scales[0, 4 * quad : 4 * quad + 4, :].bitcast(I32))
        rows = keep.tile([P, T], F32, name="rows")
        nc.vector.memset(rows[:].bitcast(I32), 0)
        nc.sync.dma_start(rows[8:9, :], rad[0:1, :])
        nc.sync.dma_start(rows[72:73, :], rf[0:1, :])

        ident = keep.tile([P, P], F32, name="ident")
        make_identity(nc, ident[:])
        seed = keep.tile([P, 16], F32, name="seed")
        nc.vector.memset(seed[:], 1.0)
        warm = reuse.tile([P, 16], F32, name="warm", offset=16384 - 64)
        nc.scalar.activation(warm[:], seed[:], ACT.Sqrt)
        words = reuse.tile([P, T], U32, name="words", offset=8192 - 32)
        nc.scalar.dma_start(words[:].bitcast(I32), x_words[0].rearrange("p n r -> p (n r)").bitcast(I32))

        q_turn = psum_t.tile([P, P], F32, tag="bank4", name="q_turn")
        nc.tensor.transpose(q_turn[:], q_flat[:], ident[:])
        q_col = keep.tile([P, n_t], F32, name="q_col")
        nc.scalar.copy(q_col[:], q_turn[:, 0:n_t])
        grouped = keep.tile([P, V, PACK], BF16, name="grouped", align_bytes=64)
        nc.scalar.copy(grouped[:].rearrange("p (c i) j -> p c j i", i=4), h_raw[:].rearrange("p j (c i) -> p c j i", i=4))

        q_bank = psum_t.tile([P, BANK], F32, tag="bank0", name="q_bank")
        for i in range(n_t):
            nc.tensor.transpose(q_bank[:, i * P : (i + 1) * P], q_col[:, i : i + 1].to_broadcast([P, P]), ident[:])
        q_row = keep.tile([P, V], F32, name="q_row")
        nc.scalar.copy(q_row[:], q_bank[:])
        q3_col = keep.tile([P, n_t], F32, name="q3_col")
        nc.scalar.activation(q3_col[:], q_col[:], ACT.Copy, scale=3.0)

        x_codes, x_planes = {}, {}

        def entries(piece):
            return offsets[:, piece * (PIECE // 16) : (piece + 1) * (PIECE // 16)]

        def pick_planes(piece):
            x_planes[piece] = reuse.tile([P, PIECE], U8, name=f"x_plane{piece}", offset=(6144, 6400, 0, 256)[piece], align_bytes=64)
            nc.vector.tensor_copy(x_planes[piece][:], planes[:].indirect(entries(piece)))

        def pick_codes(piece):
            x_codes[piece] = reuse.tile([P, PIECE], U32, name=f"x_code{piece}", offset=(1024, 16384, 4096, 5120)[piece], align_bytes=64)
            nc.vector.tensor_copy(x_codes[piece][:], words[:].indirect(entries(piece)))

        pick_planes(0)
        pick_planes(1)
        picked = reuse.tile([P, n_j, 2], F32, name="picked", offset=16384, align_bytes=64)
        for half in range(2):
            got = reuse.tile([P, BANK], F32, name=f"got{half}", offset=2048 * half, align_bytes=64)
            nc.vector.tensor_copy(got[:], rows[:].indirect(offsets[:, 32 * half : 32 * (half + 1)]))
            bank = psum_t.tile([P, 4, P], F32, tag=f"bank{1 + half}", name=f"rf_bank{half}")
            for c in range(4):
                nc.tensor.transpose(bank[:, c, :], got[:, c * P : (c + 1) * P], ident[:])
            nc.scalar.copy(picked[:, 4 * half : 4 * half + 4, :], bank[:, :, 8:73:64])
        pick_planes(2)
        pick_planes(3)
        h_codes = reuse.tile([P, V], U32, name="h_codes", offset=2048, align_bytes=64)
        h_scales = reuse.tile([P, V], U8, name="h_scales", offset=6656, align_bytes=64)
        nc.vector.quantize_mx(out=h_codes[:].bitcast(FP8X4), scales=h_scales[:], in_=grouped[:].rearrange("p t j -> p (t j)"))
        pick_codes(0)

        r_col, f_col = picked[:, :, 0], picked[:, :, 1]
        squares = keep.tile([P, n_j, 2], F32, name="squares")
        nc.scalar.activation(squares[:], picked[:], ACT.Square)
        root = reuse.tile([P, n_j], F32, name="root", offset=4096, align_bytes=64)
        nc.scalar.activation(root[:], squares[:, :, 1], ACT.Sqrt, bias=-1.0)
        warm2 = keep.tile([P, 1], F32, name="warm2")
        nc.scalar.activation(warm2[:], root[:, 0:1], ACT.Sigmoid)
        f_inv = reuse.tile([P, n_j], F32, name="f_inv", offset=5120, align_bytes=64)
        nc.vector.reciprocal(f_inv[:], f_col)
        slope = keep.tile([P, n_j], F32, name="slope")
        nc.vector.scalar_tensor_tensor(slope[:], r_col, -0.6, f_col, ALU.mult, ALU.mult)
        gap = keep.tile([P, n_j], F32, name="gap")
        nc.vector.scalar_tensor_tensor(gap[:], root[:], -0.6, r_col, ALU.mult, ALU.mult)
        shift = keep.tile([P, n_j], F32, name="shift")
        nc.vector.scalar_tensor_tensor(shift[:], root[:], 0.5, f_inv[:], ALU.mult, ALU.mult)

        gap_row = keep.tile([P, S], F32, name="gap_row")

        def spread_gap(half):
            bank = psum_t.tile([P, 4, P], F32, tag="bank3", name=f"gap_bank{half}")
            for c in range(4):
                jt = 4 * half + c
                nc.tensor.transpose(bank[:, c, :], gap[:, jt : jt + 1].to_broadcast([P, P]), ident[:])
            nc.scalar.copy(gap_row[:, half * BANK : (half + 1) * BANK], bank[:].rearrange("p c n -> p (c n)"))

        best = [[keep.tile([P, 1], F32, name=f"best{tt}_{half}") for half in range(2)] for tt in range(n_t)]
        upper, lower, drop = {}, {}, {}

        def make_drop(tt, half):
            if (tt, half) in POOL_HALVES:
                cols = slice(half * BANK, (half + 1) * BANK)
                drop[tt, half] = keep.tile([P, BANK], F32, name=f"drop{tt}_{half}")
                if (tt, half) in SCALAR_DROPS:
                    nc.scalar.activation(drop[tt, half][:], gap_row[:, cols], ACT.Identity, scale=q3_col[:, tt : tt + 1])
                else:
                    nc.gpsimd.tensor_scalar(drop[tt, half][:], gap_row[:, cols], q3_col[:, tt : tt + 1], 0.0, ALU.mult, ALU.add)

        def upper_bounds(code_tiles, query_tiles):
            width = len(query_tiles) * P
            queries = slice(query_tiles[0] * P, query_tiles[0] * P + width)
            y = psum_y.tile([P, len(code_tiles), width], F32, tag="y", name=f"y{code_tiles[0]}_{query_tiles[0]}")
            for u, jt in enumerate(code_tiles):
                piece, cols = jt // 2, slice((jt % 2) * P, (jt % 2 + 1) * P)
                nc.tensor.matmul_mx(
                    out=y[:, u, :],
                    lhsT=x_codes[piece][:, cols].bitcast(FP8X4),
                    lhsT_scale=x_planes[piece][:, cols],
                    rhs=h_codes[:, queries].bitcast(FP8X4),
                    rhs_scale=h_scales[:, queries],
                    start=True,
                    stop=True,
                )
            for u, jt in enumerate(code_tiles):
                z = ring.tile([P, width], F32, tag="z", name=f"z{jt}_{query_tiles[0]}")
                nc.vector.scalar_tensor_tensor(z[:], y[:, u, :], shift[:, jt : jt + 1], q_row[:, queries], ALU.subtract, ALU.mult)
                ub_t = ring.tile([P, width], F32, tag="ub_t", name=f"ub_t{jt}_{query_tiles[0]}")
                nc.scalar.activation(ub_t[:], z[:], ACT.Identity, bias=squares[:, jt, 0:1], scale=slope[:, jt : jt + 1])
                for w, tt in enumerate(query_tiles):
                    if jt % 4 == 0:
                        upper[tt, jt // 4] = psum_t.tile([P, 4, P], F32, tag=f"bank{((4, 0, 1, 2), (3, 4, 0, 3))[jt // 4][tt]}", name=f"ub{tt}_{jt // 4}")
                    nc.tensor.transpose(upper[tt, jt // 4][:, jt % 4, :], ub_t[:, w * P : (w + 1) * P], ident[:])

        def lower_bounds(tt, half):
            cols = slice(half * BANK, (half + 1) * BANK)
            ub = upper[tt, half][:].rearrange("p c n -> p (c n)")
            low = keep.tile([P, BANK], F32, name=f"low{tt}_{half}")
            lower[tt, half] = low
            if (tt, half) not in POOL_HALVES:
                nc.vector.scalar_tensor_tensor(low[:], gap_row[:, cols], q_col[:, tt : tt + 1], ub, ALU.mult, ALU.add)
            ub3 = ring.tile([P, BANK], F32, tag="ub3", name=f"ub3_{tt}_{half}")
            nc.vector.tensor_scalar(ub3[:], ub, 3.0, best[tt][0][:] if half else None, ALU.mult, ALU.min, accum_out=best[tt][half][:])
            if (tt, half) in POOL_HALVES:
                nc.gpsimd.tensor_tensor(low[:], ub3[:], drop[tt, half][:], ALU.add)

        def finish(tt, halves):
            for half in halves:
                res = ring.tile([P, BANK], F32, tag="res", name=f"res{tt}_{half}")
                nc.scalar.activation(
                    res[:], lower[tt, half][:], ACT.Sigmoid, bias=best[tt][1][:], scale=-1.0 if (tt, half) in POOL_HALVES else -3.0
                )
                nc.sync.dma_start(out[tt * P : (tt + 1) * P, half * BANK : (half + 1) * BANK], res[:])

        pick_codes(1)
        spread_gap(0)
        make_drop(0, 0)
        make_drop(1, 0)
        make_drop(2, 0)
        for jt in range(4):
            if jt == 2:
                pick_codes(2)
            upper_bounds((jt,), (0, 1, 2, 3))
        spread_gap(1)
        pick_codes(3)
        for pair in ((4, 5), (6, 7)):
            upper_bounds(pair, (0, 1))
        make_drop(0, 1)
        lower_bounds(0, 0)
        lower_bounds(1, 0)
        make_drop(1, 1)
        for pair in ((4, 5), (6, 7)):
            upper_bounds(pair, (2, 3))
        for tt in (0, 1):
            lower_bounds(tt, 1)
            finish(tt, (0, 1))
        lower_bounds(2, 0)
        lower_bounds(3, 0)
        for tt in (2, 3):
            lower_bounds(tt, 1)
            finish(tt, (1, 0))
